import numpy as np
CORES = [24,25,26,27,28,29,30,31,152,153,154,155,156,157,158,159]
N = 16
T, K = 128, 2
ROUTE = [[[3,15],[14,1],[1,14],[3,7],[11,8],[8,7],[0,10],[11,1],[10,5],[8,2],[2,6],[4,6],[4,6],[0,3],[1,11],[14,11],[10,14],[11,3],[10,0],[2,6],[1,4],[15,0],[14,4],[5,3],[5,13],[4,5],[15,11],[4,3],[8,9],[9,7],[11,14],[3,14],[7,3],[4,15],[9,2],[9,14],[2,11],[10,5],[14,6],[5,12],[7,10],[8,7],[15,14],[11,3],[4,11],[15,6],[14,11],[7,13],[3,10],[9,7],[10,13],[2,9],[4,2],[5,14],[13,4],[13,15],[5,15],[13,2],[7,13],[9,15],[11,14],[14,9],[9,3],[1,11],[13,8],[12,6],[8,12],[3,10],[4,5],[14,12],[9,8],[1,9],[15,8],[4,3],[2,7],[4,14],[4,11],[6,15],[4,6],[13,12],[8,10],[13,1],[5,11],[0,11],[9,5],[15,10],[14,3],[0,7],[7,14],[0,10],[9,3],[6,10],[6,13],[4,2],[6,10],[11,10],[11,5],[7,10],[1,12],[13,7],[7,11],[7,9],[10,1],[10,8],[7,5],[3,7],[4,13],[0,8],[15,5],[14,5],[5,14],[11,3],[2,8],[7,4],[10,11],[7,12],[13,0],[1,15],[10,5],[10,7],[9,2],[2,9],[15,9],[11,13],[9,2],[6,11],[8,15],[6,1]],[[0,7],[12,3],[6,15],[6,12],[2,9],[8,11],[10,0],[9,0],[1,8],[7,6],[1,4],[2,6],[3,1],[4,1],[13,0],[0,1],[10,0],[14,11],[0,14],[7,12],[9,2],[3,9],[12,1],[1,15],[12,13],[1,12],[12,11],[3,14],[9,5],[2,0],[3,7],[0,1],[4,5],[3,8],[14,5],[15,1],[14,13],[11,6],[0,3],[11,1],[9,14],[14,11],[6,8],[3,1],[10,12],[3,14],[15,11],[8,12],[3,9],[11,3],[10,12],[4,5],[2,0],[11,6],[1,4],[3,13],[8,4],[14,5],[12,9],[10,8],[13,14],[11,15],[2,15],[12,3],[8,5],[6,14],[11,14],[2,5],[0,8],[0,10],[2,10],[9,5],[15,1],[11,4],[7,13],[9,5],[10,13],[10,6],[4,11],[5,7],[14,3],[12,8],[11,0],[4,3],[8,4],[10,11],[14,2],[7,13],[14,9],[12,14],[6,0],[0,15],[12,7],[8,2],[15,5],[5,9],[14,10],[15,8],[8,9],[1,15],[3,8],[9,1],[10,3],[11,7],[7,11],[0,10],[0,5],[15,14],[13,10],[14,13],[14,7],[4,15],[11,3],[15,8],[1,0],[9,1],[3,9],[14,13],[0,10],[11,0],[5,15],[6,15],[6,11],[12,1],[7,3],[13,6],[15,9],[5,8]],[[1,14],[10,15],[10,4],[5,2],[3,14],[5,2],[7,6],[1,5],[13,0],[3,8],[11,12],[5,3],[14,3],[1,13],[15,3],[12,5],[3,12],[14,1],[3,13],[1,6],[10,0],[0,12],[15,14],[2,1],[6,13],[10,12],[4,10],[13,4],[1,3],[8,5],[14,11],[9,6],[1,10],[10,0],[1,10],[15,2],[1,3],[12,1],[3,7],[12,10],[6,2],[11,0],[2,6],[4,5],[3,7],[11,12],[2,13],[3,6],[0,3],[13,5],[4,11],[10,3],[3,13],[14,8],[0,1],[9,10],[14,8],[2,3],[0,9],[10,2],[12,3],[12,9],[8,3],[3,0],[7,10],[4,5],[6,3],[4,14],[11,10],[12,9],[5,0],[8,5],[6,11],[8,4],[5,12],[9,8],[14,3],[3,11],[12,1],[3,10],[2,7],[14,6],[5,4],[6,8],[9,14],[9,0],[15,3],[10,2],[14,10],[7,9],[12,1],[7,9],[1,5],[14,2],[7,15],[6,15],[14,13],[4,8],[11,2],[6,1],[11,5],[11,8],[7,10],[9,11],[8,10],[5,2],[8,14],[6,0],[4,3],[12,2],[8,12],[13,14],[2,9],[14,13],[2,13],[5,14],[13,15],[6,7],[4,1],[7,11],[1,8],[4,13],[11,12],[9,4],[14,11],[10,6],[13,4],[8,4]],[[0,6],[1,7],[13,2],[4,9],[5,9],[12,14],[11,1],[0,3],[15,3],[14,6],[1,8],[5,12],[7,10],[8,1],[8,0],[5,7],[1,9],[6,2],[6,15],[3,13],[4,12],[4,10],[3,11],[0,11],[13,7],[12,8],[13,6],[3,13],[13,4],[0,4],[3,10],[7,3],[10,9],[7,6],[4,13],[9,3],[3,5],[6,10],[10,1],[9,5],[3,4],[0,1],[6,10],[5,8],[10,4],[15,9],[6,1],[13,12],[8,15],[6,13],[7,5],[10,3],[7,15],[13,7],[9,7],[7,11],[15,10],[6,8],[2,1],[5,10],[12,5],[9,6],[11,15],[9,13],[7,0],[6,1],[4,0],[4,0],[2,9],[10,7],[12,11],[2,5],[11,0],[7,8],[10,5],[2,0],[1,3],[5,15],[10,12],[7,6],[13,11],[7,8],[2,15],[13,8],[2,6],[5,4],[15,9],[12,6],[0,10],[10,4],[7,9],[13,11],[4,1],[9,13],[1,4],[2,15],[12,9],[1,2],[2,1],[6,8],[7,15],[7,11],[3,8],[10,3],[10,5],[12,9],[5,10],[12,15],[4,7],[3,0],[12,15],[8,2],[8,12],[14,4],[11,1],[8,6],[4,14],[1,2],[2,11],[11,7],[15,6],[1,3],[8,9],[5,9],[2,0],[14,9],[0,13],[15,12]],[[6,1],[5,10],[12,3],[8,12],[2,14],[0,2],[11,8],[8,13],[10,11],[8,10],[1,8],[14,13],[3,12],[12,8],[5,14],[15,4],[7,5],[12,15],[2,0],[0,7],[4,7],[8,9],[9,3],[15,12],[9,10],[0,13],[15,9],[7,9],[15,11],[5,0],[5,8],[4,0],[5,6],[12,6],[6,4],[3,11],[9,0],[8,12],[5,0],[0,13],[13,6],[1,9],[6,14],[11,1],[2,12],[10,2],[4,12],[2,4],[12,10],[0,14],[6,3],[12,3],[4,14],[4,0],[15,10],[15,6],[8,14],[1,6],[13,11],[10,5],[0,14],[11,13],[3,13],[8,4],[11,15],[12,8],[4,3],[3,4],[7,9],[11,14],[9,12],[7,4],[0,12],[8,7],[10,13],[7,0],[3,4],[5,0],[3,6],[4,10],[3,15],[13,5],[7,1],[12,5],[13,11],[1,2],[6,4],[11,1],[2,7],[13,10],[7,0],[14,2],[0,11],[5,9],[11,5],[12,10],[2,11],[15,5],[2,5],[10,3],[8,6],[4,6],[4,7],[2,13],[15,3],[4,1],[15,9],[4,2],[9,1],[2,6],[11,7],[15,7],[14,12],[15,0],[13,11],[14,13],[12,2],[8,13],[1,3],[3,1],[11,0],[0,2],[8,10],[2,7],[12,14],[15,8],[4,11],[3,6]],[[7,13],[2,12],[5,1],[15,9],[3,6],[14,11],[4,3],[2,0],[13,14],[1,5],[7,15],[13,10],[2,9],[12,4],[13,1],[0,7],[4,13],[13,2],[8,15],[2,10],[5,15],[15,11],[8,9],[15,14],[10,7],[3,8],[6,9],[3,4],[15,9],[10,7],[15,14],[8,5],[15,1],[12,0],[0,1],[12,15],[14,1],[4,0],[8,9],[8,12],[2,8],[2,7],[9,3],[6,7],[9,11],[11,3],[4,5],[8,5],[12,1],[1,13],[14,5],[10,11],[11,4],[0,12],[1,6],[15,6],[1,5],[7,13],[12,15],[6,8],[10,15],[8,15],[1,5],[7,13],[10,2],[3,2],[1,0],[14,5],[14,5],[4,13],[6,1],[11,7],[12,3],[3,7],[0,11],[15,13],[3,10],[6,5],[13,9],[0,2],[9,13],[12,14],[3,0],[3,0],[3,12],[3,5],[7,0],[15,13],[13,1],[13,3],[7,12],[0,10],[8,12],[4,0],[7,12],[5,11],[12,2],[3,5],[11,8],[9,11],[12,6],[6,3],[11,13],[1,15],[5,2],[2,7],[9,0],[2,14],[12,13],[9,6],[10,6],[15,12],[14,8],[10,7],[9,4],[12,11],[2,15],[12,3],[11,4],[12,13],[14,12],[7,4],[10,7],[14,4],[15,14],[2,10],[11,5],[7,8]],[[11,15],[0,6],[8,9],[13,4],[7,2],[3,15],[4,13],[2,14],[2,8],[8,14],[0,14],[6,14],[2,5],[11,8],[11,6],[7,11],[2,1],[3,7],[8,4],[5,8],[5,3],[10,11],[3,15],[5,2],[14,7],[8,1],[10,9],[3,9],[13,4],[10,8],[8,3],[7,6],[3,9],[6,5],[14,12],[5,8],[9,14],[2,5],[7,3],[14,4],[3,7],[6,2],[7,10],[7,6],[2,6],[12,5],[2,0],[9,1],[5,2],[4,10],[4,9],[11,12],[0,12],[7,14],[7,4],[3,6],[7,1],[0,6],[11,0],[13,15],[2,1],[6,9],[8,1],[4,13],[13,7],[8,4],[12,14],[5,8],[9,10],[13,2],[11,15],[8,3],[3,13],[13,11],[10,13],[7,4],[12,7],[4,6],[11,10],[12,2],[2,6],[11,10],[6,5],[1,13],[2,9],[5,1],[3,0],[9,5],[0,13],[10,2],[11,6],[6,12],[2,6],[1,0],[0,9],[1,15],[13,3],[1,13],[5,13],[1,12],[3,1],[10,12],[9,3],[1,6],[4,11],[9,1],[2,0],[3,5],[3,6],[1,10],[11,4],[15,14],[9,6],[13,3],[5,15],[15,5],[14,11],[14,3],[7,14],[1,14],[15,10],[1,4],[2,3],[4,6],[6,1],[11,15],[11,10],[0,2]],[[9,5],[15,0],[8,2],[3,6],[15,5],[12,11],[15,12],[13,0],[5,1],[0,14],[3,13],[3,12],[13,4],[12,2],[13,6],[10,8],[1,3],[12,10],[6,8],[1,3],[0,3],[15,9],[10,9],[6,0],[14,0],[4,7],[8,2],[15,7],[6,13],[11,10],[0,10],[11,15],[0,10],[1,14],[0,10],[12,5],[13,6],[7,10],[2,1],[3,9],[8,14],[15,6],[2,0],[10,0],[9,1],[8,13],[15,13],[1,12],[1,14],[9,1],[12,8],[7,6],[14,12],[1,3],[1,5],[2,15],[12,3],[8,12],[11,10],[12,13],[14,11],[7,1],[2,13],[7,9],[2,0],[3,8],[10,8],[8,12],[8,14],[4,1],[8,0],[14,6],[1,8],[3,12],[6,3],[6,5],[15,13],[11,12],[5,6],[13,6],[11,7],[11,10],[1,7],[9,15],[1,4],[6,7],[2,3],[13,6],[0,15],[5,4],[7,5],[12,2],[14,6],[3,9],[1,9],[2,14],[15,3],[7,3],[4,8],[2,4],[8,5],[15,5],[0,7],[4,8],[12,1],[7,2],[4,13],[13,15],[0,3],[12,14],[10,9],[1,15],[12,5],[10,8],[10,7],[8,4],[4,6],[6,2],[8,5],[4,0],[3,13],[13,10],[1,15],[4,13],[5,13],[1,15],[5,2],[0,2]],[[3,11],[13,0],[3,4],[15,7],[10,13],[9,0],[14,11],[14,4],[13,15],[12,10],[10,13],[2,12],[7,10],[15,11],[2,5],[14,11],[12,5],[10,0],[10,1],[11,4],[6,3],[10,12],[9,11],[9,2],[4,13],[5,1],[2,7],[4,15],[9,14],[5,3],[9,6],[2,4],[15,4],[4,0],[11,0],[2,11],[7,5],[2,12],[9,12],[11,6],[3,1],[3,6],[12,11],[14,2],[9,4],[3,9],[6,0],[3,6],[6,1],[11,2],[8,6],[6,0],[1,12],[8,14],[4,9],[9,1],[12,0],[13,4],[5,0],[15,5],[15,7],[0,14],[13,7],[12,3],[5,3],[10,3],[13,10],[10,8],[5,14],[12,2],[10,15],[13,4],[13,5],[7,12],[6,12],[0,6],[1,11],[2,11],[11,6],[4,13],[11,9],[7,9],[2,10],[15,11],[12,11],[14,0],[8,13],[14,11],[15,10],[5,15],[1,11],[8,9],[1,0],[12,1],[0,13],[13,5],[11,2],[10,3],[6,7],[12,13],[1,4],[11,15],[10,14],[5,9],[13,15],[2,7],[1,14],[6,7],[12,1],[9,3],[7,5],[1,2],[11,9],[4,8],[5,7],[14,5],[8,14],[6,10],[15,14],[5,8],[12,7],[6,10],[4,0],[13,10],[3,4],[6,9],[5,12],[11,10]],[[5,3],[5,10],[5,2],[2,15],[6,14],[0,10],[10,0],[11,8],[9,7],[15,5],[4,2],[8,2],[1,4],[0,11],[6,5],[5,1],[7,1],[1,6],[8,2],[14,9],[6,0],[13,9],[13,8],[11,4],[8,13],[15,13],[4,2],[4,3],[3,0],[7,10],[11,1],[1,0],[8,13],[1,12],[11,8],[11,2],[10,6],[11,13],[4,8],[6,1],[9,10],[1,12],[7,2],[0,7],[9,5],[11,6],[8,10],[3,10],[14,1],[7,5],[5,9],[4,3],[6,4],[8,5],[7,8],[0,12],[2,14],[2,6],[0,9],[3,1],[13,1],[4,14],[5,3],[11,3],[10,15],[5,14],[1,4],[10,11],[13,3],[7,10],[7,14],[14,2],[11,14],[10,4],[2,11],[8,4],[8,2],[5,13],[14,1],[0,5],[14,15],[15,11],[4,1],[0,7],[6,12],[9,14],[14,3],[3,13],[6,4],[13,14],[4,7],[10,15],[14,4],[7,2],[6,2],[14,15],[4,5],[0,4],[15,13],[10,12],[15,14],[11,5],[11,5],[15,3],[5,10],[9,4],[4,7],[5,8],[7,10],[8,6],[10,7],[11,4],[15,6],[0,6],[8,13],[7,8],[14,13],[8,12],[4,13],[1,5],[11,2],[4,9],[10,0],[15,14],[1,15],[2,13],[5,11],[0,14]],[[6,14],[2,5],[1,12],[15,4],[14,9],[4,10],[5,14],[1,8],[6,4],[0,7],[12,7],[9,10],[9,0],[5,7],[12,4],[3,2],[9,8],[2,9],[3,4],[5,11],[12,9],[13,2],[7,15],[5,9],[10,14],[4,7],[2,10],[14,12],[14,3],[4,14],[7,2],[2,14],[3,11],[2,10],[2,12],[5,14],[2,12],[0,15],[14,5],[8,1],[8,3],[9,3],[6,3],[13,5],[7,13],[15,4],[13,11],[11,6],[3,2],[4,13],[4,3],[1,8],[9,1],[9,2],[12,4],[11,12],[12,3],[10,15],[5,15],[10,9],[8,13],[14,8],[3,1],[7,5],[9,0],[8,0],[1,14],[6,2],[2,8],[4,6],[7,11],[5,11],[11,12],[1,2],[15,10],[11,8],[2,8],[0,3],[6,7],[9,3],[7,6],[7,10],[6,13],[14,13],[15,7],[15,12],[9,7],[15,5],[7,11],[5,6],[3,1],[9,10],[10,2],[15,5],[1,4],[10,14],[9,15],[12,2],[14,0],[7,2],[15,6],[8,13],[5,0],[7,1],[1,5],[6,2],[2,5],[5,14],[8,9],[5,7],[1,8],[13,0],[4,10],[13,14],[7,10],[6,5],[12,1],[8,10],[9,7],[0,4],[14,1],[11,10],[5,3],[9,3],[15,11],[7,8],[0,15],[6,5]],[[11,7],[4,6],[5,15],[1,0],[0,11],[13,2],[11,4],[14,7],[9,10],[12,5],[4,15],[5,1],[15,5],[4,5],[15,10],[1,2],[12,5],[8,4],[6,2],[10,1],[9,7],[7,11],[4,7],[11,1],[8,1],[4,7],[7,2],[1,12],[8,6],[0,6],[9,15],[14,8],[7,12],[8,5],[2,6],[6,5],[3,9],[11,15],[2,4],[1,4],[11,7],[9,3],[0,3],[15,14],[0,11],[6,2],[14,3],[3,5],[11,6],[10,7],[6,13],[13,15],[12,4],[12,11],[4,2],[9,1],[2,6],[0,11],[14,6],[9,14],[8,6],[10,14],[11,3],[9,3],[12,1],[6,5],[1,10],[14,12],[0,15],[6,11],[10,6],[2,9],[5,6],[13,6],[13,3],[7,14],[7,9],[3,10],[2,1],[9,6],[8,15],[4,10],[13,11],[11,7],[5,8],[8,9],[15,12],[12,9],[1,12],[9,10],[13,0],[5,8],[14,11],[11,12],[6,1],[10,6],[8,13],[2,5],[0,13],[2,1],[13,2],[7,13],[10,13],[2,5],[1,3],[10,9],[0,8],[14,12],[8,0],[12,2],[14,15],[7,9],[11,12],[8,14],[7,9],[2,5],[14,1],[9,15],[11,8],[13,1],[14,7],[5,6],[9,0],[2,1],[0,9],[4,0],[5,14],[7,0]],[[13,1],[0,1],[9,3],[15,6],[11,12],[3,9],[11,2],[12,11],[2,10],[11,9],[8,6],[2,1],[1,8],[12,4],[12,2],[10,7],[4,5],[5,11],[13,4],[14,12],[0,10],[9,8],[2,1],[9,0],[7,0],[11,9],[11,3],[0,9],[2,0],[3,2],[12,8],[0,1],[10,14],[7,14],[15,7],[6,10],[15,2],[4,12],[13,7],[13,1],[1,11],[11,2],[10,7],[11,12],[5,11],[0,12],[7,15],[7,13],[2,11],[6,8],[9,1],[14,15],[4,11],[4,14],[5,4],[3,11],[8,9],[3,13],[11,6],[10,4],[14,2],[15,1],[14,7],[8,12],[7,6],[9,11],[10,1],[2,7],[2,0],[5,0],[5,15],[15,3],[5,15],[14,10],[7,1],[1,7],[8,0],[6,3],[2,9],[1,2],[9,11],[2,0],[10,1],[3,5],[13,15],[12,14],[7,13],[2,12],[1,11],[2,7],[6,3],[0,7],[3,1],[9,11],[9,13],[2,3],[5,9],[0,15],[5,8],[8,4],[8,11],[10,3],[4,0],[3,7],[3,4],[3,7],[13,10],[4,12],[0,7],[3,2],[10,4],[4,9],[14,8],[12,5],[13,6],[0,1],[9,11],[13,12],[12,10],[14,7],[2,3],[15,0],[14,9],[11,1],[9,13],[0,15],[9,11],[0,1]],[[5,4],[7,14],[3,15],[3,11],[14,7],[6,10],[3,0],[7,10],[4,1],[7,5],[5,8],[11,10],[5,2],[15,1],[6,1],[5,3],[12,7],[15,6],[4,8],[10,8],[3,5],[4,13],[6,8],[0,8],[7,13],[3,13],[4,12],[7,2],[7,5],[0,5],[10,3],[0,6],[7,13],[14,8],[6,0],[14,1],[5,14],[4,1],[15,1],[4,9],[11,1],[14,5],[1,8],[14,7],[15,4],[9,11],[3,4],[11,0],[8,0],[2,6],[1,12],[1,10],[6,0],[7,15],[5,13],[7,3],[4,12],[10,11],[4,2],[9,13],[12,7],[13,15],[7,8],[5,1],[4,1],[3,10],[5,9],[3,11],[15,1],[6,12],[15,8],[1,5],[12,3],[13,1],[11,13],[6,13],[12,4],[13,9],[12,13],[1,5],[12,14],[11,9],[1,5],[0,6],[10,7],[4,11],[3,13],[4,5],[12,11],[2,1],[1,10],[10,9],[6,10],[14,1],[12,10],[8,14],[9,10],[5,15],[5,2],[10,3],[1,12],[2,1],[8,7],[10,5],[9,13],[14,15],[7,12],[8,15],[13,0],[8,1],[14,2],[10,8],[15,11],[2,10],[6,3],[4,9],[0,6],[8,12],[12,4],[14,12],[5,4],[1,10],[9,10],[3,4],[12,6],[1,5],[10,15],[14,0]],[[13,4],[10,9],[4,3],[1,3],[2,9],[4,6],[4,11],[3,6],[13,5],[0,2],[15,0],[10,7],[12,11],[6,7],[0,4],[9,12],[15,1],[15,8],[11,15],[11,14],[8,2],[0,1],[6,12],[2,0],[3,0],[0,7],[6,5],[10,2],[10,6],[10,6],[4,1],[2,13],[13,14],[12,8],[10,2],[15,3],[6,12],[14,3],[11,14],[2,15],[5,10],[6,2],[5,2],[9,4],[14,3],[4,8],[14,13],[11,12],[1,9],[13,7],[12,5],[9,5],[3,2],[9,8],[8,2],[12,8],[13,0],[8,10],[4,12],[15,2],[4,14],[3,2],[4,3],[3,2],[0,3],[12,1],[4,0],[12,0],[6,4],[8,4],[2,14],[6,2],[10,6],[3,14],[15,3],[11,15],[12,0],[1,12],[13,10],[2,9],[8,11],[5,4],[0,14],[10,7],[11,2],[1,11],[3,0],[15,7],[4,14],[9,12],[5,6],[6,2],[3,6],[2,1],[2,10],[5,1],[4,7],[15,11],[2,10],[7,11],[7,5],[0,9],[2,13],[5,0],[6,10],[2,4],[13,2],[5,1],[5,15],[0,1],[8,7],[12,11],[10,0],[2,13],[11,7],[5,9],[7,11],[6,0],[0,5],[3,11],[10,13],[2,15],[0,6],[15,12],[7,8],[5,11],[1,10],[8,1]],[[7,0],[15,11],[0,15],[13,1],[10,6],[3,7],[5,10],[14,12],[5,15],[15,13],[1,4],[5,0],[12,0],[0,13],[11,4],[10,12],[4,9],[4,15],[4,15],[6,15],[7,4],[5,14],[12,7],[3,5],[6,3],[9,8],[5,2],[0,5],[6,13],[5,9],[10,5],[9,12],[7,9],[12,5],[2,7],[4,15],[14,0],[14,1],[3,5],[9,5],[1,15],[1,7],[11,10],[1,2],[1,14],[5,9],[5,1],[4,5],[0,1],[2,15],[11,1],[5,1],[7,6],[3,1],[0,5],[15,11],[7,1],[10,14],[13,6],[0,7],[3,13],[4,2],[3,12],[14,9],[11,15],[3,6],[15,13],[15,5],[12,1],[14,5],[1,10],[7,10],[8,2],[0,8],[13,1],[6,13],[0,6],[1,3],[9,10],[6,8],[4,15],[8,13],[10,13],[3,14],[14,13],[0,5],[7,12],[6,8],[13,4],[6,5],[8,7],[4,15],[8,12],[6,15],[10,9],[13,10],[7,11],[15,4],[3,12],[2,6],[4,11],[11,5],[6,0],[3,8],[5,15],[9,12],[2,6],[2,3],[6,14],[14,8],[5,4],[1,12],[8,11],[6,1],[10,15],[6,4],[10,3],[8,7],[14,8],[5,8],[12,9],[2,5],[12,13],[5,9],[15,14],[10,2],[5,15],[9,2]]]
ZW = 285
def setup_inputs(rng):
    return {"z": rng.standard_normal((N, 128, ZW), dtype=np.float32), "g": rng.random((N, 128, T * K), dtype=np.float32)}
def reference(z, g):
    y = np.zeros((N, 128, T), np.float64)
    fill = [0] * N
    for r in range(N):
        for t in range(T):
            for k, e in enumerate(ROUTE[r][t]):
                y[r][:, t] += g[r][:, t * K + k].astype(np.float64) * z[e][:, fill[e]].astype(np.float64)
                fill[e] += 1
    return {"y": y.astype(z.dtype)}

@@ -1,0 +1,96 @@
+from concourse.mybir import AluOpType
+
+SCRATCH = {
+    "zs": ("sbuf", [128, 285], "float32"),
+    "gs": ("sbuf", [128, 256], "float32"),
+    "land": ("sbuf", [128, 256], "float32"),
+    "prod": ("sbuf", [128, 256], "float32"),
+    "out": ("sbuf", [128, 128], "float32"),
+}
+SEMAPHORES = ["zl", "gl", "arrived", "sent", "vm", "va", "stored"]
+
+
+def plan(route, n, k_):
+    fill = [0] * n
+    off = [[0] * n for _ in range(n)]
+    cnt = [[0] * n for _ in range(n)]
+    zpos = []
+    for r in range(n):
+        for e in range(n):
+            off[e][r] = fill[e]
+        rows = []
+        for t in range(len(route[r])):
+            row = []
+            for e in route[r][t]:
+                row.append(fill[e])
+                fill[e] += 1
+                cnt[e][r] += 1
+            rows.append(row)
+        zpos.append(rows)
+    return off, cnt, zpos
+
+
+def bits(m):
+    return bin(m).count("1")
+
+
+def rank_program(g, core, T, topo):
+    me = T.rank_of(core)
+    if me is None:
+        return
+    route, k_, nt = T.tables["ROUTE"], T.tables["K"], T.tables["T"]
+    cores = T.cores
+    n = len(cores)
+    off, cnt, zpos = plan(route, n, k_)
+    def loffs(r):
+        o, a = [], 0
+        for e in range(n):
+            o.append(a)
+            a += cnt[e][r]
+        return o
+
+    g.sync.dma_start(T.zs[:], T.z[:]).then_inc(T.sem.zl, 16)
+    g.scalar.dma_start(T.gs[:], T.g[:]).then_inc(T.sem.gl, 16)
+
+    g.wait_ge(T.sem.zl, 16)
+    sent = 0
+    order = sorted((r for r in range(n) if r != me and cnt[me][r]),
+                   key=lambda r: (topo.host(cores[r]) == topo.host(core), (r - me) % n))
+    for r in order:
+        rid, pid = topo.addr(cores[r], core)
+        m = topo.mask(core, cores[r])
+        lo = loffs(r)[me]
+        g.remote_dma(T.land[:, lo:lo + cnt[me][r]], T.zs[:, off[me][r]:off[me][r] + cnt[me][r]],
+                     T.sem.arrived, T.sem.sent, pid, rid, m)
+        sent += bits(m)
+
+    expect = sum(bits(topo.mask(cores[e], core)) for e in range(n) if e != me and cnt[e][me])
+    lo = loffs(me)
+    v = g.vector
+    v.wait_ge(T.sem.zl, 16)
+    v.wait_ge(T.sem.gl, 16)
+    v.wait_ge(T.sem.arrived, expect)
+    nm = 0
+    for t in range(nt):
+        for k in range(k_):
+            e = route[me][t][k]
+            p = zpos[me][t][k]
+            if e == me:
+                src = T.zs[:, p:p + 1]
+            else:
+                q = lo[e] + p - off[e][me]
+                src = T.land[:, q:q + 1]
+            j = t * k_ + k
+            v.tensor_tensor(T.prod[:, j:j + 1], T.gs[:, j:j + 1], src, AluOpType.mult).then_inc(T.sem.vm, 1)
+            nm += 1
+    v.wait_ge(T.sem.vm, nm)
+    v.tensor_tensor(T.out[:], T.prod[:, 0:nt * k_:k_], T.prod[:, 1:nt * k_:k_], AluOpType.add).then_inc(T.sem.va, 1)
+    g.sync.wait_ge(T.sem.va, 1)
+    g.sync.dma_start(T.y[:], T.out[:]).then_inc(T.sem.stored, 16)
+
+    g.wait_ge(T.sem.sent, sent)
+    g.wait_ge(T.sem.arrived, expect)
+    g.wait_ge(T.sem.gl, 16)
+    g.wait_ge(T.sem.vm, nm)
+    g.wait_ge(T.sem.va, 1)
+    g.wait_ge(T.sem.stored, 16)

@@ -1,96 +1,184 @@
+from concourse.bass import DstId, RemoteDMATransfer
 from concourse.mybir import AluOpType
 
 SCRATCH = {
     "zs": ("sbuf", [128, 285], "float32"),
     "gs": ("sbuf", [128, 256], "float32"),
-    "land": ("sbuf", [128, 256], "float32"),
+    "st": ("sbuf", [128, 384], "float32"),
+    "lt": ("sbuf", [128, 256], "float32"),
     "prod": ("sbuf", [128, 256], "float32"),
     "out": ("sbuf", [128, 128], "float32"),
+    "ones": ("sbuf", [128, 128], "float32"),
+    "iota": ("sbuf", [128, 128], "float32"),
+    "tmp": ("sbuf", [128, 128], "float32"),
+    "ident": ("sbuf", [128, 128], "float32"),
+    "dr": ("dram", [248 + 285, 128, 1], "float32"),
+    "pz": ("psum", [128, 512], "float32"),
+    "res": ("psum", [128, 512], "float32"),
+    "pm": ("psum", [128, 512], "float32"),
 }
-SEMAPHORES = ["zl", "gl", "arrived", "sent", "vm", "va", "stored"]
+BASE = 248
+SEMAPHORES = ["zl", "gl", "st", "ll", "stored", "vi", "ti", "tz", "vs", "tr", "vm", "va", "arrived", "sent"]
 
 
-def plan(route, n, k_):
+def plan(route, n):
     fill = [0] * n
-    off = [[0] * n for _ in range(n)]
-    cnt = [[0] * n for _ in range(n)]
     zpos = []
     for r in range(n):
-        for e in range(n):
-            off[e][r] = fill[e]
         rows = []
         for t in range(len(route[r])):
             row = []
             for e in route[r][t]:
                 row.append(fill[e])
                 fill[e] += 1
-                cnt[e][r] += 1
             rows.append(row)
         zpos.append(rows)
-    return off, cnt, zpos
+    return zpos
 
 
-def bits(m):
-    return bin(m).count("1")
+def landing(route, r, k_):
+    items = [(k, t) for k in range(k_) for t in range(len(route[r])) if route[r][t][k] != r]
+    idx = {}
+    for i in range(len(items)):
+        idx[items[i]] = i
+    return idx
+
+
+def slot(i, h):
+    return 2 * i if i < h else 2 * (i - h) + 1
 
 
 def rank_program(g, core, T, topo):
     me = T.rank_of(core)
     if me is None:
         return
-    route, k_, nt = T.tables["ROUTE"], T.tables["K"], T.tables["T"]
+    route, k_, nt, zw = T.tables["ROUTE"], T.tables["K"], T.tables["T"], T.tables["ZW"]
     cores = T.cores
     n = len(cores)
-    off, cnt, zpos = plan(route, n, k_)
-    def loffs(r):
-        o, a = [], 0
-        for e in range(n):
-            o.append(a)
-            a += cnt[e][r]
-        return o
+    S = T.sem
+    v, pe, sy, sc = g.vector, g.tensor, g.sync, g.scalar
+    zpos = plan(route, n)
+    nj = 3
+    zc = zw // nj
+    assert k_ == 2 and nt == 128 and zc * nj == zw and zc <= 128
 
-    g.sync.dma_start(T.zs[:], T.z[:]).then_inc(T.sem.zl, 16)
-    g.scalar.dma_start(T.gs[:], T.g[:]).then_inc(T.sem.gl, 16)
+    sy.dma_start(T.zs[:], T.z[:]).then_inc(S.zl, 16)
+    sc.dma_start(T.gs[:], T.g[:]).then_inc(S.gl, 16)
 
-    g.wait_ge(T.sem.zl, 16)
+    vi = [0]
+
+    def step(ins):
+        ins.then_inc(S.vi, 1)
+        vi[0] += 1
+
+    step(v.memset(T.ones[:], 1.0))
+    step(v.memset(T.iota[:, 0:1], 0.0))
+    s = 1
+    while s < 128:
+        step(v.memset(T.tmp[:, s:2 * s], float(s)))
+        s *= 2
+    s = 1
+    while s < 128:
+        v.wait_ge(S.vi, vi[0])
+        step(v.tensor_tensor(T.iota[:, s:2 * s], T.iota[:, 0:s], T.tmp[:, s:2 * s], AluOpType.add))
+        s *= 2
+    pe.wait_ge(S.vi, vi[0])
+    pe.matmul(T.pm[:, 0:128], T.iota[0:1, :], T.ones[0:1, :], True, True).then_inc(S.ti, 1)
+    v.wait_ge(S.vi, vi[0])
+    v.wait_ge(S.ti, 1)
+    step(v.tensor_tensor(T.tmp[:], T.pm[:, 0:128], T.iota[:], AluOpType.subtract))
+    v.wait_ge(S.vi, vi[0])
+    step(v.tensor_tensor(T.ident[:], T.tmp[:], T.tmp[:], AluOpType.mult))
+    v.wait_ge(S.vi, vi[0])
+    step(v.tensor_tensor(T.tmp[:], T.ident[:], T.ones[:], AluOpType.min))
+    v.wait_ge(S.vi, vi[0])
+    step(v.tensor_tensor(T.ident[:], T.ones[:], T.tmp[:], AluOpType.subtract))
+    nvi = vi[0]
+
+    pe.wait_ge(S.vi, nvi)
+    pe.wait_ge(S.zl, 16)
+    for j in range(nj):
+        pe.matmul(T.pz[0:zc, j * 128:(j + 1) * 128], T.zs[:, j:zw:nj], T.ident[:], True, True).then_inc(S.tz, 1)
+    v.wait_ge(S.tz, nj)
+    v.tensor_copy(T.st[0:zc, :], T.pz[0:zc, 0:nj * 128]).then_inc(S.vs, 1)
+    sy.wait_ge(S.vs, 1)
+    sy.dma_start(T.dr[BASE:BASE + zw], T.st[0:zc, :]).then_inc(S.st, 16)
+
+    far, near = [], []
+    for r in range(n):
+        if r == me:
+            continue
+        idx = landing(route, r, k_)
+        h = (len(idx) + 1) // 2
+        lst = near if topo.mask(core, cores[r]) == 0xFFFF else far
+        m = 0
+        for t in range(nt):
+            for k in range(k_):
+                if route[r][t][k] == me:
+                    lst.append((m, r, BASE + zpos[r][t][k], BASE - len(idx) + slot(idx[(k, t)], h)))
+                    m += 1
+    far.sort()
+    near.sort()
+    g.wait_ge(S.st, 16)
     sent = 0
-    order = sorted((r for r in range(n) if r != me and cnt[me][r]),
-                   key=lambda r: (topo.host(cores[r]) == topo.host(core), (r - me) % n))
-    for r in order:
-        rid, pid = topo.addr(cores[r], core)
-        m = topo.mask(core, cores[r])
-        lo = loffs(r)[me]
-        g.remote_dma(T.land[:, lo:lo + cnt[me][r]], T.zs[:, off[me][r]:off[me][r] + cnt[me][r]],
-                     T.sem.arrived, T.sem.sent, pid, rid, m)
-        sent += bits(m)
+    while far or near:
+        batch = far[:8]
+        far = far[8:]
+        room = 16 - len(batch)
+        batch = batch + near[:room]
+        near = near[room:]
+        trs = []
+        for eng in range(len(batch)):
+            _m, r, c, sl = batch[eng]
+            rid, pid = topo.addr(cores[r], core)
+            trs.append(RemoteDMATransfer(dst_ids=[DstId(rid=rid, pnc=pid)], dma_engine_mask=1 << eng,
+                                         remote_sem=S.arrived, src=T.dr[c], dst=T.dr[sl]))
+        g.remote_dma_fused(trs, local_sem=S.sent)
+        sent += len(batch)
 
-    expect = sum(bits(topo.mask(cores[e], core)) for e in range(n) if e != me and cnt[e][me])
-    lo = loffs(me)
-    v = g.vector
-    v.wait_ge(T.sem.zl, 16)
-    v.wait_ge(T.sem.gl, 16)
-    v.wait_ge(T.sem.arrived, expect)
+    idx = landing(route, me, k_)
+    expect = len(idx)
+    h = (expect + 1) // 2
+    assert expect <= BASE
+    sy.wait_ge(S.st, 16)
+    sy.wait_ge(S.arrived, expect)
+    sy.dma_start(T.lt[0:h, :], T.dr[BASE - expect:BASE - expect + 2 * h]).then_inc(S.ll, 16)
+    pe.wait_ge(S.ll, 16)
+    for j in range(2):
+        kj = h if j == 0 else expect - h
+        pe.matmul(T.res[:, j * h:j * h + kj], T.lt[0:kj, j * 128:(j + 1) * 128], T.ident[0:kj, 0:kj],
+                  True, True).then_inc(S.tr, 1)
+    v.wait_ge(S.zl, 16)
+    v.wait_ge(S.gl, 16)
     nm = 0
-    for t in range(nt):
-        for k in range(k_):
-            e = route[me][t][k]
-            p = zpos[me][t][k]
-            if e == me:
-                src = T.zs[:, p:p + 1]
-            else:
-                q = lo[e] + p - off[e][me]
-                src = T.land[:, q:q + 1]
-            j = t * k_ + k
-            v.tensor_tensor(T.prod[:, j:j + 1], T.gs[:, j:j + 1], src, AluOpType.mult).then_inc(T.sem.vm, 1)
+    for k in range(k_):
+        for t in range(nt):
+            if (k, t) not in idx:
+                p = zpos[me][t][k]
+                j = t * k_ + k
+                v.tensor_tensor(T.prod[:, k * nt + t:k * nt + t + 1], T.zs[:, p:p + 1], T.gs[:, j:j + 1],
+                                AluOpType.mult).then_inc(S.vm, 1)
+                nm += 1
+    v.wait_ge(S.tr, 2)
+    for k in range(k_):
+        t = 0
+        while t < nt:
+            if (k, t) not in idx:
+                t += 1
+                continue
+            t1 = t
+            while t1 < nt and (k, t1) in idx:
+                t1 += 1
+            i0 = idx[(k, t)]
+            v.tensor_tensor(T.prod[:, k * nt + t:k * nt + t1], T.res[:, i0:i0 + t1 - t],
+                            T.gs[:, t * k_ + k:(t1 - 1) * k_ + k + 1:k_], AluOpType.mult).then_inc(S.vm, 1)
             nm += 1
-    v.wait_ge(T.sem.vm, nm)
-    v.tensor_tensor(T.out[:], T.prod[:, 0:nt * k_:k_], T.prod[:, 1:nt * k_:k_], AluOpType.add).then_inc(T.sem.va, 1)
-    g.sync.wait_ge(T.sem.va, 1)
-    g.sync.dma_start(T.y[:], T.out[:]).then_inc(T.sem.stored, 16)
+            t = t1
+    v.wait_ge(S.vm, nm)
+    v.tensor_tensor(T.out[:], T.prod[:, 0:nt], T.prod[:, nt:2 * nt], AluOpType.add).then_inc(S.va, 1)
+    sy.wait_ge(S.va, 1)
+    sy.dma_start(T.y[:], T.out[:]).then_inc(S.stored, 16)
 
-    g.wait_ge(T.sem.sent, sent)
-    g.wait_ge(T.sem.arrived, expect)
-    g.wait_ge(T.sem.gl, 16)
-    g.wait_ge(T.sem.vm, nm)
-    g.wait_ge(T.sem.va, 1)
-    g.wait_ge(T.sem.stored, 16)
+    g.wait_ge(S.sent, sent)
+    g.wait_ge(S.arrived, expect)
+    g.wait_ge(S.stored, 16)

from concourse.bass import DstId, RemoteDMATransfer
from concourse.mybir import AluOpType

SCRATCH = {
    "zs": ("sbuf", [128, 285], "float32"),
    "gs": ("sbuf", [128, 256], "float32"),
    "st": ("sbuf", [128, 384], "float32"),
    "lt": ("sbuf", [128, 256], "float32"),
    "prod": ("sbuf", [128, 256], "float32"),
    "out": ("sbuf", [128, 128], "float32"),
    "ones": ("sbuf", [128, 128], "float32"),
    "iota": ("sbuf", [128, 128], "float32"),
    "tmp": ("sbuf", [128, 128], "float32"),
    "ident": ("sbuf", [128, 128], "float32"),
    "dr": ("dram", [248 + 285, 128, 1], "float32"),
    "pz": ("psum", [128, 512], "float32"),
    "res": ("psum", [128, 512], "float32"),
    "pm": ("psum", [128, 512], "float32"),
}
BASE = 248
SEMAPHORES = ["zl", "gl", "st", "ll", "stored", "vi", "ti", "tz", "vs", "tr", "vm", "va", "arrived", "sent"]


def plan(route, n):
    fill = [0] * n
    zpos = []
    for r in range(n):
        rows = []
        for t in range(len(route[r])):
            row = []
            for e in route[r][t]:
                row.append(fill[e])
                fill[e] += 1
            rows.append(row)
        zpos.append(rows)
    return zpos


def landing(route, r, k_):
    items = [(k, t) for k in range(k_) for t in range(len(route[r])) if route[r][t][k] != r]
    idx = {}
    for i in range(len(items)):
        idx[items[i]] = i
    return idx


def slot(i, h):
    return 2 * i if i < h else 2 * (i - h) + 1


def rank_program(g, core, T, topo):
    me = T.rank_of(core)
    if me is None:
        return
    route, k_, nt, zw = T.tables["ROUTE"], T.tables["K"], T.tables["T"], T.tables["ZW"]
    cores = T.cores
    n = len(cores)
    S = T.sem
    v, pe, sy, sc = g.vector, g.tensor, g.sync, g.scalar
    zpos = plan(route, n)
    nj = 3
    zc = zw // nj
    assert k_ == 2 and nt == 128 and zc * nj == zw and zc <= 128

    sy.dma_start(T.zs[:], T.z[:]).then_inc(S.zl, 16)
    sc.dma_start(T.gs[:], T.g[:]).then_inc(S.gl, 16)

    vi = [0]

    def step(ins):
        ins.then_inc(S.vi, 1)
        vi[0] += 1

    step(v.memset(T.ones[:], 1.0))
    step(v.memset(T.iota[:, 0:1], 0.0))
    s = 1
    while s < 128:
        step(v.memset(T.tmp[:, s:2 * s], float(s)))
        s *= 2
    s = 1
    while s < 128:
        v.wait_ge(S.vi, vi[0])
        step(v.tensor_tensor(T.iota[:, s:2 * s], T.iota[:, 0:s], T.tmp[:, s:2 * s], AluOpType.add))
        s *= 2
    pe.wait_ge(S.vi, vi[0])
    pe.matmul(T.pm[:, 0:128], T.iota[0:1, :], T.ones[0:1, :], True, True).then_inc(S.ti, 1)
    v.wait_ge(S.vi, vi[0])
    v.wait_ge(S.ti, 1)
    step(v.tensor_tensor(T.tmp[:], T.pm[:, 0:128], T.iota[:], AluOpType.subtract))
    v.wait_ge(S.vi, vi[0])
    step(v.tensor_tensor(T.ident[:], T.tmp[:], T.tmp[:], AluOpType.mult))
    v.wait_ge(S.vi, vi[0])
    step(v.tensor_tensor(T.tmp[:], T.ident[:], T.ones[:], AluOpType.min))
    v.wait_ge(S.vi, vi[0])
    step(v.tensor_tensor(T.ident[:], T.ones[:], T.tmp[:], AluOpType.subtract))
    nvi = vi[0]

    pe.wait_ge(S.vi, nvi)
    pe.wait_ge(S.zl, 16)
    for j in range(nj):
        pe.matmul(T.pz[0:zc, j * 128:(j + 1) * 128], T.zs[:, j:zw:nj], T.ident[:], True, True).then_inc(S.tz, 1)
    v.wait_ge(S.tz, nj)
    v.tensor_copy(T.st[0:zc, :], T.pz[0:zc, 0:nj * 128]).then_inc(S.vs, 1)
    sy.wait_ge(S.vs, 1)
    sy.dma_start(T.dr[BASE:BASE + zw], T.st[0:zc, :]).then_inc(S.st, 16)

    far, near = [], []
    for r in range(n):
        if r == me:
            continue
        idx = landing(route, r, k_)
        h = (len(idx) + 1) // 2
        lst = near if topo.mask(core, cores[r]) == 0xFFFF else far
        m = 0
        for t in range(nt):
            for k in range(k_):
                if route[r][t][k] == me:
                    lst.append((m, r, BASE + zpos[r][t][k], BASE - len(idx) + slot(idx[(k, t)], h)))
                    m += 1
    far.sort()
    near.sort()
    g.wait_ge(S.st, 16)
    sent = 0
    while far or near:
        batch = far[:8]
        far = far[8:]
        room = 16 - len(batch)
        batch = batch + near[:room]
        near = near[room:]
        trs = []
        for eng in range(len(batch)):
            _m, r, c, sl = batch[eng]
            rid, pid = topo.addr(cores[r], core)
            trs.append(RemoteDMATransfer(dst_ids=[DstId(rid=rid, pnc=pid)], dma_engine_mask=1 << eng,
                                         remote_sem=S.arrived, src=T.dr[c], dst=T.dr[sl]))
        g.remote_dma_fused(trs, local_sem=S.sent)
        sent += len(batch)

    idx = landing(route, me, k_)
    expect = len(idx)
    h = (expect + 1) // 2
    assert expect <= BASE
    sy.wait_ge(S.st, 16)
    sy.wait_ge(S.arrived, expect)
    sy.dma_start(T.lt[0:h, :], T.dr[BASE - expect:BASE - expect + 2 * h]).then_inc(S.ll, 16)
    pe.wait_ge(S.ll, 16)
    for j in range(2):
        kj = h if j == 0 else expect - h
        pe.matmul(T.res[:, j * h:j * h + kj], T.lt[0:kj, j * 128:(j + 1) * 128], T.ident[0:kj, 0:kj],
                  True, True).then_inc(S.tr, 1)
    v.wait_ge(S.zl, 16)
    v.wait_ge(S.gl, 16)
    nm = 0
    for k in range(k_):
        for t in range(nt):
            if (k, t) not in idx:
                p = zpos[me][t][k]
                j = t * k_ + k
                v.tensor_tensor(T.prod[:, k * nt + t:k * nt + t + 1], T.zs[:, p:p + 1], T.gs[:, j:j + 1],
                                AluOpType.mult).then_inc(S.vm, 1)
                nm += 1
    v.wait_ge(S.tr, 2)
    for k in range(k_):
        t = 0
        while t < nt:
            if (k, t) not in idx:
                t += 1
                continue
            t1 = t
            while t1 < nt and (k, t1) in idx:
                t1 += 1
            i0 = idx[(k, t)]
            v.tensor_tensor(T.prod[:, k * nt + t:k * nt + t1], T.res[:, i0:i0 + t1 - t],
                            T.gs[:, t * k_ + k:(t1 - 1) * k_ + k + 1:k_], AluOpType.mult).then_inc(S.vm, 1)
            nm += 1
            t = t1
    v.wait_ge(S.vm, nm)
    v.tensor_tensor(T.out[:], T.prod[:, 0:nt], T.prod[:, nt:2 * nt], AluOpType.add).then_inc(S.va, 1)
    sy.wait_ge(S.va, 1)
    sy.dma_start(T.y[:], T.out[:]).then_inc(S.stored, 16)

    g.wait_ge(S.sent, sent)
    g.wait_ge(S.arrived, expect)
    g.wait_ge(S.stored, 16)
